import numpy as np
import ml_dtypes


def mxq(x, axis, fmt="e4m3"):
    dtype, down = {"e4m3": (ml_dtypes.float8_e4m3fn, 7), "e5m2": (ml_dtypes.float8_e5m2, 14)}[fmt]
    v = np.moveaxis(np.asarray(x, np.float32).astype(ml_dtypes.bfloat16).astype(np.float64), axis, -1)
    blocks = v.reshape(v.shape[:-1] + (-1, 32))
    amax = np.abs(blocks).max(-1, keepdims=True)
    byte = np.maximum(np.where(amax > 0, np.frexp(amax)[1] - 1 + 127, 0) - down, 1)
    scale = np.exp2(byte - 127.0)
    codes = (blocks / scale).astype(np.float32).astype(dtype).astype(np.float64)
    return np.moveaxis((codes * scale).reshape(v.shape), -1, axis)


WIDE = False


def mx_kscale(k):
    if not WIDE:
        return np.ones(k)
    levels = np.array([10, -10, 5, -5, 0])
    if k % 512:
        return np.exp2(np.random.permutation(np.resize(levels, k // 32))).repeat(32)
    a = np.empty((k // 512, 16))
    for p in range(k // 512):
        a[p, :8] = np.random.permutation(np.resize(levels, 8))
        for g in range(8):
            far = levels[np.abs(levels - a[p, g]) >= 10]
            a[p, g + 8] = far[np.random.randint(len(far))]
    return np.exp2(a.ravel()).repeat(32)


def f64(x):
    return np.asarray(x).astype(np.float64)


def striped(idx):
    return np.tile(idx.reshape(-1, 16).T, (8, 1)).astype(np.uint16)


def unstriped(offs):
    return offs[:16].T.reshape(-1).astype(np.int64)


def pack_weight(w):
    k, n = w.shape
    w = f64(np.asarray(w, np.float32).astype(ml_dtypes.bfloat16)).reshape(k // 32, 32, n)
    amax = np.abs(w).max(1)
    byte = np.clip(np.where(amax > 0, np.frexp(amax)[1] - 1 + 127 - 7, 1), 1, 254)
    scaled = (w * np.exp2(127.0 - byte)[:, None, :]).reshape(k, n).astype(np.float32)
    words = np.ascontiguousarray(scaled.reshape(k // 512, 128, 4, n).transpose(0, 1, 3, 2)).astype(ml_dtypes.float8_e4m3fn).view(np.uint8)
    return words, np.ascontiguousarray(byte.astype(np.uint8).reshape(k // 512, 16, n))


def unpack_weight(words, scales):
    g, p, n, _ = words.shape
    vals = np.ascontiguousarray(words).view(ml_dtypes.float8_e4m3fn).astype(np.float64) * np.repeat(np.exp2(scales.astype(np.float64) - 127.0), 8, axis=1)[..., None]
    return vals.transpose(0, 1, 3, 2).reshape(g * 512, n)


def sigmoid(v):
    return 1.0 / (1.0 + np.exp(-np.maximum(v, -700.0)))


K, T, S, N, V = 512, 2048, 512, 128, 256
P = 2 ** 7


def setup_inputs():
    n = np.random.standard_normal
    s = mx_kscale(K)[:, None]
    packed_xT = pack_weight(n((K, T)) * s)
    return {
        "x_words": packed_xT[0],
        "x_scales": packed_xT[1],
        "w1": (n((K, N)) / np.sqrt(K) / s).astype(np.float32),
        "w2": (n((K, N)) / np.sqrt(K) / s).astype(np.float32),
        "w3": (n((K, N)) / np.sqrt(K) / s).astype(np.float32),
        "air": (np.random.uniform(0.8, 1.0, (N, 1))).astype(np.float32),
        "tmin": (np.tile(np.random.uniform(0.35, 0.65, V), (P, 1))).astype(np.float32),
        "nair": (-np.random.uniform(0.8, 1.0, (N, 1))).astype(np.float32),
        "offs": striped(np.random.permutation(T)[:S]),
        "pos1": striped(np.random.permutation(S)[:V]),
        "pos2": striped(np.random.permutation(S)[:V]),
        "pos3": striped(np.random.permutation(S)[:V]),
        "cen": striped(np.random.permutation(S)[:V]),
    }


def reference(x_words, x_scales, w1, w2, w3, air, tmin, nair, offs, pos1, pos2, pos3, cen):
    xq = unpack_weight(x_words, x_scales)[:, unstriped(offs)]
    yr = mxq(f64(w1), 0, "e4m3").T @ xq
    red = sigmoid(yr + 1.5)
    yg = mxq(f64(w2), 0, "e4m3").T @ xq
    grn = sigmoid(yg + 1.5)
    yb = mxq(f64(w3), 0, "e4m3").T @ xq
    blu = sigmoid(yb + 1.5)
    dark = np.minimum(np.minimum(red, grn), blu)
    mn = np.minimum(np.minimum(np.minimum(dark[:, unstriped(cen)], dark[:, unstriped(pos1)]), dark[:, unstriped(pos2)]), dark[:, unstriped(pos3)])
    tr = np.maximum(-1.0 * (0.95 * (mn / (0.2 * mn + f64(air)))) + 1.0, f64(tmin)[:1])
    return (red[:, unstriped(cen)] + f64(nair)) / tr + f64(air)

@@ -1,0 +1,255 @@
+import math
+from contextlib import ExitStack
+
+import concourse.mybir as mybir
+
+K, T, S, N, V = 512, 2048, 512, 128, 256
+P = 128
+FLOPS = 3 * 2 * K * N * S
+
+F32 = mybir.dt.float32
+BF16 = mybir.dt.bfloat16
+I32 = mybir.dt.int32
+U32 = mybir.dt.uint32
+U16 = mybir.dt.uint16
+U8 = mybir.dt.uint8
+FP8X4 = mybir.dt.float8_e4m3fn_x4
+ALU = mybir.AluOpType
+ACT = mybir.ActivationFunctionType
+
+ROOT = math.sqrt(0.15)
+SHIFT = 0.275 / ROOT
+CHUNKS = (128, 128)
+XPARTS = 2
+
+
+def tile_picked_ydehz_red_p_kernel(
+    tc, x_words, x_scales, w1, w2, w3, air, tmin, nair, offs, pos1, pos2, pos3, cen, out
+):
+    nc = tc.nc
+    with ExitStack() as ctx:
+        sb = ctx.enter_context(tc.tile_pool(name="sb", bufs=1))
+        ps = ctx.enter_context(tc.psum_pool(name="ps", bufs=1))
+
+        offs_t = sb.tile([P, S // 16], U16, name="offs_t")
+        nc.sync.dma_start(offs_t[:], offs)
+        xs = sb.tile([P, T], U8, name="xs", align_bytes=64)
+        nc.vector.memset(xs[:].bitcast(I32), 0)
+
+        raws = [sb.tile([P, 4, N], F32, name="raw%d" % i) for i in range(3)]
+
+        def load_w(i, w):
+            nc.sync.dma_start(raws[i][:], w.rearrange("(p j) m -> p j m", j=4))
+
+        load_w(0, w1)
+        for q in range(4):
+            nc.sync.dma_start(
+                xs[32 * q : 32 * q + 4, :].bitcast(I32),
+                x_scales[0, 4 * q : 4 * q + 4, :].bitcast(I32),
+            )
+        xw = sb.tile([P, T], U32, name="xw", align_bytes=64)
+        nc.sync.dma_start(
+            xw[:].bitcast(I32), x_words[0].rearrange("p n t -> p (n t)").bitcast(I32)
+        )
+        load_w(1, w2)
+        load_w(2, w3)
+        cen_t = sb.tile([P, V // 16], U16, name="cen_t")
+        nc.sync.dma_start(cen_t[:], cen)
+        lists = [cen_t]
+        for i, pos in enumerate((pos1, pos2, pos3)):
+            pos_t = sb.tile([P, V // 16], U16, name="pos_t%d" % i)
+            nc.sync.dma_start(pos_t[:], pos)
+            lists.append(pos_t)
+        air_t = sb.tile([P, 1], F32, name="air_t")
+        nc.sync.dma_start(air_t[:], air)
+        nair_t = sb.tile([P, 1], F32, name="nair_t")
+        nc.sync.dma_start(nair_t[:], nair)
+        tmin_t = sb.tile([P, V], F32, name="tmin_t")
+        nc.sync.dma_start(tmin_t[:], tmin)
+
+        grouped, codes, scales = [], [], []
+        for i in range(3):
+            grouped.append(sb.tile([P, N, 4], BF16, name="grouped%d" % i, align_bytes=64))
+            codes.append(sb.tile([P, N], U32, name="codes%d" % i, align_bytes=64))
+            scales.append(sb.tile([P, N], U8, name="scales%d" % i, align_bytes=64))
+
+        def interleave(i, copy):
+            copy(grouped[i][:], raws[i][:].rearrange("p j m -> p m j"))
+
+        def quantize(i):
+            nc.vector.quantize_mx(
+                out=codes[i][:].bitcast(FP8X4),
+                scales=scales[i][:],
+                in_=grouped[i][:].rearrange("p m j -> p (m j)"),
+            )
+
+        interleave(0, nc.scalar.copy)
+        quantize(0)
+        gs = sb.tile([P, S], U8, name="gs", align_bytes=64)
+        nc.vector.tensor_copy(gs[:], xs[:].indirect(offs_t[:]))
+        width = S // XPARTS
+        gws = []
+        for h in range(XPARTS):
+            gw = sb.tile([P, width], U32, name="gw%d" % h, align_bytes=64)
+            nc.vector.tensor_copy(
+                gw[:], xw[:].indirect(offs_t[:, h * width // 16 : (h + 1) * width // 16])
+            )
+            gws.append(gw)
+        interleave(1, nc.scalar.copy)
+        quantize(1)
+        interleave(2, nc.vector.tensor_copy)
+        quantize(2)
+
+        g_col = sb.tile([P, 1], F32, name="g_col")
+        nc.gpsimd.tensor_scalar(g_col[:], air_t[:], air_t[:], 1.0 + SHIFT * SHIFT, ALU.mult, ALU.mult)
+        b_col = sb.tile([P, 1], F32, name="b_col")
+        nc.gpsimd.tensor_scalar(b_col[:], air_t[:], SHIFT, 0.0, ALU.mult, ALU.add)
+
+        red_win = sb.tile([P, S], F32, name="red_win")
+        two = sb.tile([P, S], F32, name="two")
+        dark_win = sb.tile([P, S], F32, name="dark_win")
+        red = sb.tile([P, V], F32, name="red")
+        for i in range(3):
+            for h in range(XPARTS):
+                cols = slice(h * width, (h + 1) * width)
+                acc = ps.tile([P, width], F32, name="acc%d_%d" % (i, h))
+                nc.tensor.matmul_mx(
+                    out=acc[:],
+                    lhsT=codes[i][:].bitcast(FP8X4),
+                    lhsT_scale=scales[i][:],
+                    rhs=gws[h][:].bitcast(FP8X4),
+                    rhs_scale=gs[:, cols],
+                    start=True,
+                    stop=True,
+                )
+                if i == 0:
+                    nc.scalar.activation(red_win[:, cols], acc[:], ACT.Copy, bias=1.5)
+                elif i == 1:
+                    nc.vector.scalar_tensor_tensor(
+                        two[:, cols], acc[:], 1.5, red_win[:, cols], ALU.add, ALU.min
+                    )
+                else:
+                    nc.vector.scalar_tensor_tensor(
+                        dark_win[:, cols], acc[:], 1.5, two[:, cols], ALU.add, ALU.min
+                    )
+            if i == 0:
+                nc.scalar.activation(red[:], red_win[:].indirect(cen_t[:]), ACT.Sigmoid)
+
+        widths = [128,128]
+        starts = [sum(widths[:c]) for c in range(len(widths))]
+        tiles = {}
+
+        def t(name, c, half=False):
+            if (name, c) not in tiles:
+                n = widths[c] // 2 if half else widths[c]
+                tiles[(name, c)] = sb.tile([P, n], F32, name="%s%d" % (name, c))
+            return tiles[(name, c)][:]
+
+        def two_of(ap):
+            return ap.rearrange("p (a b) -> p a b", a=2)
+
+        def cols(c):
+            return slice(starts[c], starts[c] + widths[c])
+
+        def win(l, c):
+            return dark_win[:].indirect(lists[l][:, starts[c] // 16 : (starts[c] + widths[c]) // 16])
+
+        def sg(dst, l, c):
+            nc.scalar.activation(t(dst, c), win(l, c), ACT.Sigmoid)
+
+        def vg(dst, l, c):
+            nc.vector.tensor_copy(t(dst, c), win(l, c))
+
+        def mi(dst, a, b, c):
+            nc.vector.tensor_tensor(t(dst, c), t(a, c), t(b, c), ALU.min)
+
+        def sig(dst, a, c):
+            nc.scalar.activation(t(dst, c), t(a, c), ACT.Sigmoid)
+
+        def dd(c):
+            nc.scalar.activation(t("dd", c), t("mn", c), ACT.Square, bias=air_t[:], scale=0.2)
+
+        def qq(c):
+            nc.scalar.activation(t("qq", c), t("mn", c), ACT.Square, bias=b_col[:], scale=ROOT)
+
+        def bound(c):
+            nc.vector.scalar_tensor_tensor(
+                t("bound", c), t("dd", c), -1.0, tmin_t[:, cols(c)], ALU.mult, ALU.mult
+            )
+
+        def den(c):
+            nc.vector.scalar_tensor_tensor(
+                t("den", c), t("qq", c), g_col[:], t("bound", c), ALU.subtract, ALU.min
+            )
+
+        def num(c):
+            nc.vector.scalar_tensor_tensor(
+                t("num", c), red[:, cols(c)], nair_t[:], t("dd", c), ALU.add, ALU.mult
+            )
+
+        def num2(c):
+            nc.vector.scalar_tensor_tensor(
+                t("num2", c), t("den", c), air_t[:], t("num", c), ALU.mult, ALU.subtract
+            )
+
+        def prod(c):
+            d = two_of(t("den", c))
+            nc.vector.tensor_tensor(t("prod", c, True), d[:, 0, :], d[:, 1, :], ALU.mult)
+
+        def cof(c):
+            nc.vector.tensor_tensor(
+                two_of(t("cof", c)), two_of(t("num2", c)), two_of(t("den", c))[:, ::-1, :], ALU.mult
+            )
+
+        def inv(c):
+            nc.vector.reciprocal(t("inv", c, True), t("prod", c, True))
+
+        def quo(c):
+            nc.vector.tensor_tensor(
+                two_of(t("quo", c)),
+                two_of(t("cof", c)),
+                t("inv", c, True).unsqueeze(1).to_broadcast([P, 2, widths[c] // 2]),
+                ALU.mult,
+            )
+
+        def store(c, eng):
+            eng.dma_start(out[:, cols(c)], t("quo", c))
+
+        vg("g2", 2, 0)
+        vg("g3", 3, 0)
+        sg("s0", 0, 0)
+        sg("s1", 1, 0)
+        vg("g2", 2, 1)
+        vg("g3", 3, 1)
+        sg("s0", 0, 1)
+        sg("s1", 1, 1)
+        mi("g23", "g2", "g3", 0)
+        mi("g23", "g2", "g3", 1)
+        sig("s23", "g23", 0)
+        sig("s23", "g23", 1)
+        mi("m01", "s0", "s1", 0)
+        mi("m01", "s0", "s1", 1)
+        mi("mn", "m01", "s23", 0)
+        mi("mn", "m01", "s23", 1)
+        dd(0)
+        qq(0)
+        dd(1)
+        qq(1)
+        bound(0)
+        bound(1)
+        den(0)
+        den(1)
+        num(0)
+        num(1)
+        prod(0)
+        prod(1)
+        num2(0)
+        num2(1)
+        inv(0)
+        inv(1)
+        cof(0)
+        cof(1)
+        quo(0)
+        quo(1)
+        store(0, nc.sync)
+        store(1, nc.sync)

@@ -35,6 +35,10 @@ def tile_picked_ydehz_red_p_kernel(
         nc.sync.dma_start(offs_t[:], offs)
         xs = sb.tile([P, T], U8, name="xs", align_bytes=64)
         nc.vector.memset(xs[:].bitcast(I32), 0)
+        warm = sb.tile([P, 1], F32, name="warm")
+        warm2 = sb.tile([P, 1], F32, name="warm2")
+        nc.gpsimd.memset(warm[:], 0.0)
+        nc.scalar.activation(warm2[:], warm[:], ACT.Sigmoid)
 
         raws = [sb.tile([P, 4, N], F32, name="raw%d" % i) for i in range(3)]
 

@@ -31,8 +31,6 @@ def tile_picked_ydehz_red_p_kernel(
         sb = ctx.enter_context(tc.tile_pool(name="sb", bufs=1))
         ps = ctx.enter_context(tc.psum_pool(name="ps", bufs=1))
 
-        offs_t = sb.tile([P, S // 16], U16, name="offs_t")
-        nc.sync.dma_start(offs_t[:], offs)
         xs = sb.tile([P, T], U8, name="xs", align_bytes=64)
         nc.vector.memset(xs[:].bitcast(I32), 0)
         warm = sb.tile([P, 1], F32, name="warm")
@@ -46,15 +44,17 @@ def tile_picked_ydehz_red_p_kernel(
             nc.sync.dma_start(raws[i][:], w.rearrange("(p j) m -> p j m", j=4))
 
         load_w(0, w1)
-        for q in range(4):
+        offs_t = sb.tile([P, S // 16], U16, name="offs_t")
+        nc.sync.dma_start(offs_t[:], offs)
+        xw = sb.tile([P, T], U32, name="xw", align_bytes=64)
+        words = x_words[0].rearrange("p n t -> p (n t)").bitcast(I32)
+        nc.sync.dma_start(xw[:, :512].bitcast(I32), words[:, :512])
+        for q in (0, 2, 1, 3):
             nc.sync.dma_start(
                 xs[32 * q : 32 * q + 4, :].bitcast(I32),
                 x_scales[0, 4 * q : 4 * q + 4, :].bitcast(I32),
             )
-        xw = sb.tile([P, T], U32, name="xw", align_bytes=64)
-        nc.sync.dma_start(
-            xw[:].bitcast(I32), x_words[0].rearrange("p n t -> p (n t)").bitcast(I32)
-        )
+        nc.sync.dma_start(xw[:, 512:].bitcast(I32), words[:, 512:])
         load_w(1, w2)
         load_w(2, w3)
         cen_t = sb.tile([P, V // 16], U16, name="cen_t")
@@ -77,8 +77,12 @@ def tile_picked_ydehz_red_p_kernel(
             codes.append(sb.tile([P, N], U32, name="codes%d" % i, align_bytes=64))
             scales.append(sb.tile([P, N], U8, name="scales%d" % i, align_bytes=64))
 
-        def interleave(i, copy):
-            copy(grouped[i][:], raws[i][:].rearrange("p j m -> p m j"))
+        def interleave(i, split):
+            src = raws[i][:].rearrange("p j m -> p m j")
+            if split > 0:
+                nc.scalar.copy(grouped[i][:, :split, :], src[:, :split, :])
+            if split < N:
+                nc.vector.tensor_copy(grouped[i][:, split:, :], src[:, split:, :])
 
         def quantize(i):
             nc.vector.quantize_mx(
@@ -87,7 +91,7 @@ def tile_picked_ydehz_red_p_kernel(
                 in_=grouped[i][:].rearrange("p m j -> p (m j)"),
             )
 
-        interleave(0, nc.scalar.copy)
+        interleave(0, 128)
         quantize(0)
         gs = sb.tile([P, S], U8, name="gs", align_bytes=64)
         nc.vector.tensor_copy(gs[:], xs[:].indirect(offs_t[:]))
@@ -99,9 +103,9 @@ def tile_picked_ydehz_red_p_kernel(
                 gw[:], xw[:].indirect(offs_t[:, h * width // 16 : (h + 1) * width // 16])
             )
             gws.append(gw)
-        interleave(1, nc.scalar.copy)
+        interleave(1, 128)
         quantize(1)
-        interleave(2, nc.vector.tensor_copy)
+        interleave(2, 0)
         quantize(2)
 
         g_col = sb.tile([P, 1], F32, name="g_col")

@@ -5,6 +5,8 @@ import concourse.mybir as mybir
 
 K, T, S, N, V = 512, 2048, 512, 128, 256
 P = 128
+PACK = 4
+LIST_ROWS = 16
 FLOPS = 3 * 2 * K * N * S
 
 F32 = mybir.dt.float32
@@ -17,10 +19,15 @@ FP8X4 = mybir.dt.float8_e4m3fn_x4
 ALU = mybir.AluOpType
 ACT = mybir.ActivationFunctionType
 
+OFFSET = 1.5
 ROOT = math.sqrt(0.15)
 SHIFT = 0.275 / ROOT
-CHUNKS = (128, 128)
-XPARTS = 2
+
+HALVES = (0, 1)
+S_HALF = S // 2
+V_HALF = V // 2
+PAIRS = V_HALF // 2
+LEAD = T // 4
 
 
 def tile_picked_ydehz_red_p_kernel(
@@ -28,236 +35,190 @@ def tile_picked_ydehz_red_p_kernel(
 ):
     nc = tc.nc
     with ExitStack() as ctx:
-        sb = ctx.enter_context(tc.tile_pool(name="sb", bufs=1))
-        ps = ctx.enter_context(tc.psum_pool(name="ps", bufs=1))
+        sbuf = ctx.enter_context(tc.tile_pool(name="sbuf", bufs=1))
+        psum = ctx.enter_context(tc.psum_pool(name="psum", bufs=1))
 
-        xs = sb.tile([P, T], U8, name="xs", align_bytes=64)
-        nc.vector.memset(xs[:].bitcast(I32), 0)
-        warm = sb.tile([P, 1], F32, name="warm")
-        warm2 = sb.tile([P, 1], F32, name="warm2")
-        nc.gpsimd.memset(warm[:], 0.0)
-        nc.scalar.activation(warm2[:], warm[:], ACT.Sigmoid)
+        def load(name, source, dtype):
+            tile = sbuf.tile(list(source.shape), dtype, name=name)
+            nc.sync.dma_start(tile[:], source)
+            return tile
 
-        raws = [sb.tile([P, 4, N], F32, name="raw%d" % i) for i in range(3)]
+        def load_weights(name, w):
+            return load(name, w.rearrange("(p j) m -> p j m", j=PACK), F32)
 
-        def load_w(i, w):
-            nc.sync.dma_start(raws[i][:], w.rearrange("(p j) m -> p j m", j=4))
+        all_scales = sbuf.tile([P, T], U8, name="all_scales", align_bytes=64)
+        nc.vector.memset(all_scales[:].bitcast(I32), 0)
 
-        load_w(0, w1)
-        offs_t = sb.tile([P, S // 16], U16, name="offs_t")
-        nc.sync.dma_start(offs_t[:], offs)
-        xw = sb.tile([P, T], U32, name="xw", align_bytes=64)
-        words = x_words[0].rearrange("p n t -> p (n t)").bitcast(I32)
-        nc.sync.dma_start(xw[:, :512].bitcast(I32), words[:, :512])
+        warm_in = sbuf.tile([P, 1], F32, name="warm_in")
+        warm_out = sbuf.tile([P, 1], F32, name="warm_out")
+        nc.gpsimd.memset(warm_in[:], 0.0)
+        nc.scalar.activation(warm_out[:], warm_in[:], ACT.Sigmoid)
+
+        w1_rows = load_weights("w1_rows", w1)
+        offs_list = load("offs_list", offs, U16)
+        all_words = sbuf.tile([P, T], U32, name="all_words", align_bytes=64)
+        words_hbm = x_words[0].rearrange("p n j -> p (n j)").bitcast(I32)
+        nc.sync.dma_start(all_words[:, :LEAD].bitcast(I32), words_hbm[:, :LEAD])
         for q in (0, 2, 1, 3):
             nc.sync.dma_start(
-                xs[32 * q : 32 * q + 4, :].bitcast(I32),
+                all_scales[32 * q : 32 * q + 4, :].bitcast(I32),
                 x_scales[0, 4 * q : 4 * q + 4, :].bitcast(I32),
             )
-        nc.sync.dma_start(xw[:, 512:].bitcast(I32), words[:, 512:])
-        load_w(1, w2)
-        load_w(2, w3)
-        cen_t = sb.tile([P, V // 16], U16, name="cen_t")
-        nc.sync.dma_start(cen_t[:], cen)
-        lists = [cen_t]
-        for i, pos in enumerate((pos1, pos2, pos3)):
-            pos_t = sb.tile([P, V // 16], U16, name="pos_t%d" % i)
-            nc.sync.dma_start(pos_t[:], pos)
-            lists.append(pos_t)
-        air_t = sb.tile([P, 1], F32, name="air_t")
-        nc.sync.dma_start(air_t[:], air)
-        nair_t = sb.tile([P, 1], F32, name="nair_t")
-        nc.sync.dma_start(nair_t[:], nair)
-        tmin_t = sb.tile([P, V], F32, name="tmin_t")
-        nc.sync.dma_start(tmin_t[:], tmin)
+        nc.sync.dma_start(all_words[:, LEAD:].bitcast(I32), words_hbm[:, LEAD:])
+        w2_rows = load_weights("w2_rows", w2)
+        w3_rows = load_weights("w3_rows", w3)
+        cen_list = load("cen_list", cen, U16)
+        pos1_list = load("pos1_list", pos1, U16)
+        pos2_list = load("pos2_list", pos2, U16)
+        pos3_list = load("pos3_list", pos3, U16)
+        nair_col = load("nair_col", nair, F32)
+        tmin_rows = load("tmin_rows", tmin, F32)
+        air_col = load("air_col", air, F32)
 
-        grouped, codes, scales = [], [], []
-        for i in range(3):
-            grouped.append(sb.tile([P, N, 4], BF16, name="grouped%d" % i, align_bytes=64))
-            codes.append(sb.tile([P, N], U32, name="codes%d" % i, align_bytes=64))
-            scales.append(sb.tile([P, N], U8, name="scales%d" % i, align_bytes=64))
-
-        def interleave(i, split):
-            src = raws[i][:].rearrange("p j m -> p m j")
-            if split > 0:
-                nc.scalar.copy(grouped[i][:, :split, :], src[:, :split, :])
-            if split < N:
-                nc.vector.tensor_copy(grouped[i][:, split:, :], src[:, split:, :])
-
-        def quantize(i):
+        def quantize(name, rows, copy):
+            grouped = sbuf.tile([P, N, PACK], BF16, name=name + "_grouped", align_bytes=64)
+            copy(
+                grouped[:].rearrange("p (c e) j -> p c j e", e=4),
+                rows[:].rearrange("p j (c e) -> p c j e", e=4),
+            )
+            words = sbuf.tile([P, N], U32, name=name + "_words", align_bytes=64)
+            scales = sbuf.tile([P, N], U8, name=name + "_scales", align_bytes=64)
             nc.vector.quantize_mx(
-                out=codes[i][:].bitcast(FP8X4),
-                scales=scales[i][:],
-                in_=grouped[i][:].rearrange("p m j -> p (m j)"),
+                out=words[:].bitcast(FP8X4),
+                scales=scales[:],
+                in_=grouped[:].rearrange("p m j -> p (m j)"),
             )
+            return words, scales
 
-        interleave(0, 128)
-        quantize(0)
-        gs = sb.tile([P, S], U8, name="gs", align_bytes=64)
-        nc.vector.tensor_copy(gs[:], xs[:].indirect(offs_t[:]))
-        width = S // XPARTS
-        gws = []
-        for h in range(XPARTS):
-            gw = sb.tile([P, width], U32, name="gw%d" % h, align_bytes=64)
-            nc.vector.tensor_copy(
-                gw[:], xw[:].indirect(offs_t[:, h * width // 16 : (h + 1) * width // 16])
+        w1_mx = quantize("w1", w1_rows, nc.scalar.copy)
+
+        picked_scales = sbuf.tile([P, S], U8, name="picked_scales", align_bytes=64)
+        nc.vector.tensor_copy(picked_scales[:], all_scales[:].indirect(offs_list[:]))
+        picked_words = []
+        for h in HALVES:
+            entries = offs_list[:, h * S_HALF // LIST_ROWS : (h + 1) * S_HALF // LIST_ROWS]
+            words = sbuf.tile([P, S_HALF], U32, name="picked_words%d" % h, align_bytes=64)
+            nc.vector.tensor_copy(words[:], all_words[:].indirect(entries))
+            picked_words.append(words)
+
+        w2_mx = quantize("w2", w2_rows, nc.scalar.copy)
+        w3_mx = quantize("w3", w3_rows, nc.vector.tensor_copy)
+
+        square_rest = sbuf.tile([P, 1], F32, name="square_rest")
+        nc.gpsimd.tensor_scalar(
+            square_rest[:], air_col[:], air_col[:], 1.0 + SHIFT * SHIFT, ALU.mult, ALU.mult
+        )
+        square_shift = sbuf.tile([P, 1], F32, name="square_shift")
+        nc.gpsimd.tensor_scalar(square_shift[:], air_col[:], SHIFT, 0.0, ALU.mult, ALU.add)
+
+        def product(name, w_mx, h):
+            words, scales = w_mx
+            acc = psum.tile([P, S_HALF], F32, name="%s%d" % (name, h))
+            nc.tensor.matmul_mx(
+                out=acc[:],
+                lhsT=words[:].bitcast(FP8X4),
+                lhsT_scale=scales[:],
+                rhs=picked_words[h][:].bitcast(FP8X4),
+                rhs_scale=picked_scales[:, h * S_HALF : (h + 1) * S_HALF],
+                start=True,
+                stop=True,
             )
-            gws.append(gw)
-        interleave(1, 128)
-        quantize(1)
-        interleave(2, 0)
-        quantize(2)
+            return acc
 
-        g_col = sb.tile([P, 1], F32, name="g_col")
-        nc.gpsimd.tensor_scalar(g_col[:], air_t[:], air_t[:], 1.0 + SHIFT * SHIFT, ALU.mult, ALU.mult)
-        b_col = sb.tile([P, 1], F32, name="b_col")
-        nc.gpsimd.tensor_scalar(b_col[:], air_t[:], SHIFT, 0.0, ALU.mult, ALU.add)
-
-        red_win = sb.tile([P, S], F32, name="red_win")
-        two = sb.tile([P, S], F32, name="two")
-        dark_win = sb.tile([P, S], F32, name="dark_win")
-        red = sb.tile([P, V], F32, name="red")
-        for i in range(3):
-            for h in range(XPARTS):
-                cols = slice(h * width, (h + 1) * width)
-                acc = ps.tile([P, width], F32, name="acc%d_%d" % (i, h))
-                nc.tensor.matmul_mx(
-                    out=acc[:],
-                    lhsT=codes[i][:].bitcast(FP8X4),
-                    lhsT_scale=scales[i][:],
-                    rhs=gws[h][:].bitcast(FP8X4),
-                    rhs_scale=gs[:, cols],
-                    start=True,
-                    stop=True,
+        red_arg = sbuf.tile([P, S], F32, name="red_arg")
+        red_green_arg = sbuf.tile([P, S], F32, name="red_green_arg")
+        dark_arg = sbuf.tile([P, S], F32, name="dark_arg")
+        red = sbuf.tile([P, V], F32, name="red")
+        picked = [slice(h * S_HALF, (h + 1) * S_HALF) for h in HALVES]
+        for h in HALVES:
+            acc = product("yr", w1_mx, h)
+            nc.scalar.activation(red_arg[:, picked[h]], acc[:], ACT.Copy, bias=OFFSET)
+        nc.scalar.activation(red[:], red_arg[:].indirect(cen_list[:]), ACT.Sigmoid)
+        for name, w_mx, lesser, so_far in (
+            ("yg", w2_mx, red_green_arg, red_arg),
+            ("yb", w3_mx, dark_arg, red_green_arg),
+        ):
+            for h in HALVES:
+                acc = product(name, w_mx, h)
+                nc.vector.scalar_tensor_tensor(
+                    lesser[:, picked[h]], acc[:], OFFSET, so_far[:, picked[h]], ALU.add, ALU.min
                 )
-                if i == 0:
-                    nc.scalar.activation(red_win[:, cols], acc[:], ACT.Copy, bias=1.5)
-                elif i == 1:
-                    nc.vector.scalar_tensor_tensor(
-                        two[:, cols], acc[:], 1.5, red_win[:, cols], ALU.add, ALU.min
-                    )
-                else:
-                    nc.vector.scalar_tensor_tensor(
-                        dark_win[:, cols], acc[:], 1.5, two[:, cols], ALU.add, ALU.min
-                    )
-            if i == 0:
-                nc.scalar.activation(red[:], red_win[:].indirect(cen_t[:]), ACT.Sigmoid)
 
-        widths = [128,128]
-        starts = [sum(widths[:c]) for c in range(len(widths))]
-        tiles = {}
+        def halves(name, width=V_HALF):
+            return [sbuf.tile([P, width], F32, name="%s%d" % (name, h)) for h in HALVES]
 
-        def t(name, c, half=False):
-            if (name, c) not in tiles:
-                n = widths[c] // 2 if half else widths[c]
-                tiles[(name, c)] = sb.tile([P, n], F32, name="%s%d" % (name, c))
-            return tiles[(name, c)][:]
+        def dark_at(list_tile, h):
+            entries = list_tile[:, h * V_HALF // LIST_ROWS : (h + 1) * V_HALF // LIST_ROWS]
+            return dark_arg[:].indirect(entries)
 
-        def two_of(ap):
-            return ap.rearrange("p (a b) -> p a b", a=2)
+        def paired(tile):
+            return tile[:].rearrange("p (a v) -> p a v", a=2)
 
-        def cols(c):
-            return slice(starts[c], starts[c] + widths[c])
+        outputs = [slice(h * V_HALF, (h + 1) * V_HALF) for h in HALVES]
 
-        def win(l, c):
-            return dark_win[:].indirect(lists[l][:, starts[c] // 16 : (starts[c] + widths[c]) // 16])
+        arg2, arg3 = halves("arg2"), halves("arg3")
+        dark_cen, dark1 = halves("dark_cen"), halves("dark1")
+        for h in HALVES:
+            nc.vector.tensor_copy(arg2[h][:], dark_at(pos2_list, h))
+            nc.vector.tensor_copy(arg3[h][:], dark_at(pos3_list, h))
+            nc.scalar.activation(dark_cen[h][:], dark_at(cen_list, h), ACT.Sigmoid)
+            nc.scalar.activation(dark1[h][:], dark_at(pos1_list, h), ACT.Sigmoid)
 
-        def sg(dst, l, c):
-            nc.scalar.activation(t(dst, c), win(l, c), ACT.Sigmoid)
+        arg23, dark23 = halves("arg23"), halves("dark23")
+        dark_cen1, mn = halves("dark_cen1"), halves("mn")
+        for h in HALVES:
+            nc.vector.tensor_tensor(arg23[h][:], arg2[h][:], arg3[h][:], ALU.min)
+        for h in HALVES:
+            nc.scalar.activation(dark23[h][:], arg23[h][:], ACT.Sigmoid)
+        for h in HALVES:
+            nc.vector.tensor_tensor(dark_cen1[h][:], dark_cen[h][:], dark1[h][:], ALU.min)
+        for h in HALVES:
+            nc.vector.tensor_tensor(mn[h][:], dark_cen1[h][:], dark23[h][:], ALU.min)
 
-        def vg(dst, l, c):
-            nc.vector.tensor_copy(t(dst, c), win(l, c))
-
-        def mi(dst, a, b, c):
-            nc.vector.tensor_tensor(t(dst, c), t(a, c), t(b, c), ALU.min)
-
-        def sig(dst, a, c):
-            nc.scalar.activation(t(dst, c), t(a, c), ACT.Sigmoid)
-
-        def dd(c):
-            nc.scalar.activation(t("dd", c), t("mn", c), ACT.Square, bias=air_t[:], scale=0.2)
-
-        def qq(c):
-            nc.scalar.activation(t("qq", c), t("mn", c), ACT.Square, bias=b_col[:], scale=ROOT)
-
-        def bound(c):
-            nc.vector.scalar_tensor_tensor(
-                t("bound", c), t("dd", c), -1.0, tmin_t[:, cols(c)], ALU.mult, ALU.mult
+        d_sq, square = halves("d_sq"), halves("square")
+        for h in HALVES:
+            nc.scalar.activation(d_sq[h][:], mn[h][:], ACT.Square, bias=air_col[:], scale=0.2)
+            nc.scalar.activation(
+                square[h][:], mn[h][:], ACT.Square, bias=square_shift[:], scale=ROOT
             )
 
-        def den(c):
+        bound, den = halves("bound"), halves("den")
+        for h in HALVES:
             nc.vector.scalar_tensor_tensor(
-                t("den", c), t("qq", c), g_col[:], t("bound", c), ALU.subtract, ALU.min
+                bound[h][:], d_sq[h][:], -1.0, tmin_rows[:, outputs[h]], ALU.mult, ALU.mult
+            )
+        for h in HALVES:
+            nc.vector.scalar_tensor_tensor(
+                den[h][:], square[h][:], square_rest[:], bound[h][:], ALU.subtract, ALU.min
             )
 
-        def num(c):
+        haze, num, den_pair = halves("haze"), halves("num"), halves("den_pair", PAIRS)
+        for h in HALVES:
             nc.vector.scalar_tensor_tensor(
-                t("num", c), red[:, cols(c)], nair_t[:], t("dd", c), ALU.add, ALU.mult
+                haze[h][:], red[:, outputs[h]], nair_col[:], d_sq[h][:], ALU.add, ALU.mult
             )
-
-        def num2(c):
-            nc.vector.scalar_tensor_tensor(
-                t("num2", c), t("den", c), air_t[:], t("num", c), ALU.mult, ALU.subtract
-            )
-
-        def prod(c):
-            d = two_of(t("den", c))
-            nc.vector.tensor_tensor(t("prod", c, True), d[:, 0, :], d[:, 1, :], ALU.mult)
-
-        def cof(c):
+        for h in HALVES:
             nc.vector.tensor_tensor(
-                two_of(t("cof", c)), two_of(t("num2", c)), two_of(t("den", c))[:, ::-1, :], ALU.mult
+                den_pair[h][:], den[h][:, :PAIRS], den[h][:, PAIRS:], ALU.mult
+            )
+        for h in HALVES:
+            nc.vector.scalar_tensor_tensor(
+                num[h][:], den[h][:], air_col[:], haze[h][:], ALU.mult, ALU.subtract
             )
 
-        def inv(c):
-            nc.vector.reciprocal(t("inv", c, True), t("prod", c, True))
-
-        def quo(c):
+        inverse, num_partner, result = halves("inverse", PAIRS), halves("num_partner"), halves("result")
+        for h in HALVES:
+            nc.vector.reciprocal(inverse[h][:], den_pair[h][:])
+        for h in HALVES:
             nc.vector.tensor_tensor(
-                two_of(t("quo", c)),
-                two_of(t("cof", c)),
-                t("inv", c, True).unsqueeze(1).to_broadcast([P, 2, widths[c] // 2]),
+                paired(num_partner[h]), paired(num[h]), paired(den[h])[:, ::-1, :], ALU.mult
+            )
+        for h in HALVES:
+            nc.vector.tensor_tensor(
+                paired(result[h]),
+                paired(num_partner[h]),
+                inverse[h][:].unsqueeze(1).to_broadcast([P, 2, PAIRS]),
                 ALU.mult,
             )
-
-        def store(c, eng):
-            eng.dma_start(out[:, cols(c)], t("quo", c))
-
-        vg("g2", 2, 0)
-        vg("g3", 3, 0)
-        sg("s0", 0, 0)
-        sg("s1", 1, 0)
-        vg("g2", 2, 1)
-        vg("g3", 3, 1)
-        sg("s0", 0, 1)
-        sg("s1", 1, 1)
-        mi("g23", "g2", "g3", 0)
-        mi("g23", "g2", "g3", 1)
-        sig("s23", "g23", 0)
-        sig("s23", "g23", 1)
-        mi("m01", "s0", "s1", 0)
-        mi("m01", "s0", "s1", 1)
-        mi("mn", "m01", "s23", 0)
-        mi("mn", "m01", "s23", 1)
-        dd(0)
-        qq(0)
-        dd(1)
-        qq(1)
-        bound(0)
-        bound(1)
-        den(0)
-        den(1)
-        num(0)
-        num(1)
-        prod(0)
-        prod(1)
-        num2(0)
-        num2(1)
-        inv(0)
-        inv(1)
-        cof(0)
-        cof(1)
-        quo(0)
-        quo(1)
-        store(0, nc.sync)
-        store(1, nc.sync)
+        for h in HALVES:
+            nc.sync.dma_start(out[:, outputs[h]], result[h][:])

import math
from contextlib import ExitStack

import concourse.mybir as mybir

K, T, S, N, V = 512, 2048, 512, 128, 256
P = 128
PACK = 4
LIST_ROWS = 16
FLOPS = 3 * 2 * K * N * S

F32 = mybir.dt.float32
BF16 = mybir.dt.bfloat16
I32 = mybir.dt.int32
U32 = mybir.dt.uint32
U16 = mybir.dt.uint16
U8 = mybir.dt.uint8
FP8X4 = mybir.dt.float8_e4m3fn_x4
ALU = mybir.AluOpType
ACT = mybir.ActivationFunctionType

OFFSET = 1.5
ROOT = math.sqrt(0.15)
SHIFT = 0.275 / ROOT

HALVES = (0, 1)
S_HALF = S // 2
V_HALF = V // 2
PAIRS = V_HALF // 2
LEAD = T // 4


def tile_picked_ydehz_red_p_kernel(
    tc, x_words, x_scales, w1, w2, w3, air, tmin, nair, offs, pos1, pos2, pos3, cen, out
):
    nc = tc.nc
    with ExitStack() as ctx:
        sbuf = ctx.enter_context(tc.tile_pool(name="sbuf", bufs=1))
        psum = ctx.enter_context(tc.psum_pool(name="psum", bufs=1))

        def load(name, source, dtype):
            tile = sbuf.tile(list(source.shape), dtype, name=name)
            nc.sync.dma_start(tile[:], source)
            return tile

        def load_weights(name, w):
            return load(name, w.rearrange("(p j) m -> p j m", j=PACK), F32)

        all_scales = sbuf.tile([P, T], U8, name="all_scales", align_bytes=64)
        nc.vector.memset(all_scales[:].bitcast(I32), 0)

        warm_in = sbuf.tile([P, 1], F32, name="warm_in")
        warm_out = sbuf.tile([P, 1], F32, name="warm_out")
        nc.gpsimd.memset(warm_in[:], 0.0)
        nc.scalar.activation(warm_out[:], warm_in[:], ACT.Sigmoid)

        w1_rows = load_weights("w1_rows", w1)
        offs_list = load("offs_list", offs, U16)
        all_words = sbuf.tile([P, T], U32, name="all_words", align_bytes=64)
        words_hbm = x_words[0].rearrange("p n j -> p (n j)").bitcast(I32)
        nc.sync.dma_start(all_words[:, :LEAD].bitcast(I32), words_hbm[:, :LEAD])
        for q in (0, 2, 1, 3):
            nc.sync.dma_start(
                all_scales[32 * q : 32 * q + 4, :].bitcast(I32),
                x_scales[0, 4 * q : 4 * q + 4, :].bitcast(I32),
            )
        nc.sync.dma_start(all_words[:, LEAD:].bitcast(I32), words_hbm[:, LEAD:])
        w2_rows = load_weights("w2_rows", w2)
        w3_rows = load_weights("w3_rows", w3)
        cen_list = load("cen_list", cen, U16)
        pos1_list = load("pos1_list", pos1, U16)
        pos2_list = load("pos2_list", pos2, U16)
        pos3_list = load("pos3_list", pos3, U16)
        nair_col = load("nair_col", nair, F32)
        tmin_rows = load("tmin_rows", tmin, F32)
        air_col = load("air_col", air, F32)

        def quantize(name, rows, copy):
            grouped = sbuf.tile([P, N, PACK], BF16, name=name + "_grouped", align_bytes=64)
            copy(
                grouped[:].rearrange("p (c e) j -> p c j e", e=4),
                rows[:].rearrange("p j (c e) -> p c j e", e=4),
            )
            words = sbuf.tile([P, N], U32, name=name + "_words", align_bytes=64)
            scales = sbuf.tile([P, N], U8, name=name + "_scales", align_bytes=64)
            nc.vector.quantize_mx(
                out=words[:].bitcast(FP8X4),
                scales=scales[:],
                in_=grouped[:].rearrange("p m j -> p (m j)"),
            )
            return words, scales

        w1_mx = quantize("w1", w1_rows, nc.scalar.copy)

        picked_scales = sbuf.tile([P, S], U8, name="picked_scales", align_bytes=64)
        nc.vector.tensor_copy(picked_scales[:], all_scales[:].indirect(offs_list[:]))
        picked_words = []
        for h in HALVES:
            entries = offs_list[:, h * S_HALF // LIST_ROWS : (h + 1) * S_HALF // LIST_ROWS]
            words = sbuf.tile([P, S_HALF], U32, name="picked_words%d" % h, align_bytes=64)
            nc.vector.tensor_copy(words[:], all_words[:].indirect(entries))
            picked_words.append(words)

        w2_mx = quantize("w2", w2_rows, nc.scalar.copy)
        w3_mx = quantize("w3", w3_rows, nc.vector.tensor_copy)

        square_rest = sbuf.tile([P, 1], F32, name="square_rest")
        nc.gpsimd.tensor_scalar(
            square_rest[:], air_col[:], air_col[:], 1.0 + SHIFT * SHIFT, ALU.mult, ALU.mult
        )
        square_shift = sbuf.tile([P, 1], F32, name="square_shift")
        nc.gpsimd.tensor_scalar(square_shift[:], air_col[:], SHIFT, 0.0, ALU.mult, ALU.add)

        def product(name, w_mx, h):
            words, scales = w_mx
            acc = psum.tile([P, S_HALF], F32, name="%s%d" % (name, h))
            nc.tensor.matmul_mx(
                out=acc[:],
                lhsT=words[:].bitcast(FP8X4),
                lhsT_scale=scales[:],
                rhs=picked_words[h][:].bitcast(FP8X4),
                rhs_scale=picked_scales[:, h * S_HALF : (h + 1) * S_HALF],
                start=True,
                stop=True,
            )
            return acc

        red_arg = sbuf.tile([P, S], F32, name="red_arg")
        red_green_arg = sbuf.tile([P, S], F32, name="red_green_arg")
        dark_arg = sbuf.tile([P, S], F32, name="dark_arg")
        red = sbuf.tile([P, V], F32, name="red")
        picked = [slice(h * S_HALF, (h + 1) * S_HALF) for h in HALVES]
        for h in HALVES:
            acc = product("yr", w1_mx, h)
            nc.scalar.activation(red_arg[:, picked[h]], acc[:], ACT.Copy, bias=OFFSET)
        nc.scalar.activation(red[:], red_arg[:].indirect(cen_list[:]), ACT.Sigmoid)
        for name, w_mx, lesser, so_far in (
            ("yg", w2_mx, red_green_arg, red_arg),
            ("yb", w3_mx, dark_arg, red_green_arg),
        ):
            for h in HALVES:
                acc = product(name, w_mx, h)
                nc.vector.scalar_tensor_tensor(
                    lesser[:, picked[h]], acc[:], OFFSET, so_far[:, picked[h]], ALU.add, ALU.min
                )

        def halves(name, width=V_HALF):
            return [sbuf.tile([P, width], F32, name="%s%d" % (name, h)) for h in HALVES]

        def dark_at(list_tile, h):
            entries = list_tile[:, h * V_HALF // LIST_ROWS : (h + 1) * V_HALF // LIST_ROWS]
            return dark_arg[:].indirect(entries)

        def paired(tile):
            return tile[:].rearrange("p (a v) -> p a v", a=2)

        outputs = [slice(h * V_HALF, (h + 1) * V_HALF) for h in HALVES]

        arg2, arg3 = halves("arg2"), halves("arg3")
        dark_cen, dark1 = halves("dark_cen"), halves("dark1")
        for h in HALVES:
            nc.vector.tensor_copy(arg2[h][:], dark_at(pos2_list, h))
            nc.vector.tensor_copy(arg3[h][:], dark_at(pos3_list, h))
            nc.scalar.activation(dark_cen[h][:], dark_at(cen_list, h), ACT.Sigmoid)
            nc.scalar.activation(dark1[h][:], dark_at(pos1_list, h), ACT.Sigmoid)

        arg23, dark23 = halves("arg23"), halves("dark23")
        dark_cen1, mn = halves("dark_cen1"), halves("mn")
        for h in HALVES:
            nc.vector.tensor_tensor(arg23[h][:], arg2[h][:], arg3[h][:], ALU.min)
        for h in HALVES:
            nc.scalar.activation(dark23[h][:], arg23[h][:], ACT.Sigmoid)
        for h in HALVES:
            nc.vector.tensor_tensor(dark_cen1[h][:], dark_cen[h][:], dark1[h][:], ALU.min)
        for h in HALVES:
            nc.vector.tensor_tensor(mn[h][:], dark_cen1[h][:], dark23[h][:], ALU.min)

        d_sq, square = halves("d_sq"), halves("square")
        for h in HALVES:
            nc.scalar.activation(d_sq[h][:], mn[h][:], ACT.Square, bias=air_col[:], scale=0.2)
            nc.scalar.activation(
                square[h][:], mn[h][:], ACT.Square, bias=square_shift[:], scale=ROOT
            )

        bound, den = halves("bound"), halves("den")
        for h in HALVES:
            nc.vector.scalar_tensor_tensor(
                bound[h][:], d_sq[h][:], -1.0, tmin_rows[:, outputs[h]], ALU.mult, ALU.mult
            )
        for h in HALVES:
            nc.vector.scalar_tensor_tensor(
                den[h][:], square[h][:], square_rest[:], bound[h][:], ALU.subtract, ALU.min
            )

        haze, num, den_pair = halves("haze"), halves("num"), halves("den_pair", PAIRS)
        for h in HALVES:
            nc.vector.scalar_tensor_tensor(
                haze[h][:], red[:, outputs[h]], nair_col[:], d_sq[h][:], ALU.add, ALU.mult
            )
        for h in HALVES:
            nc.vector.tensor_tensor(
                den_pair[h][:], den[h][:, :PAIRS], den[h][:, PAIRS:], ALU.mult
            )
        for h in HALVES:
            nc.vector.scalar_tensor_tensor(
                num[h][:], den[h][:], air_col[:], haze[h][:], ALU.mult, ALU.subtract
            )

        inverse, num_partner, result = halves("inverse", PAIRS), halves("num_partner"), halves("result")
        for h in HALVES:
            nc.vector.reciprocal(inverse[h][:], den_pair[h][:])
        for h in HALVES:
            nc.vector.tensor_tensor(
                paired(num_partner[h]), paired(num[h]), paired(den[h])[:, ::-1, :], ALU.mult
            )
        for h in HALVES:
            nc.vector.tensor_tensor(
                paired(result[h]),
                paired(num_partner[h]),
                inverse[h][:].unsqueeze(1).to_broadcast([P, 2, PAIRS]),
                ALU.mult,
            )
        for h in HALVES:
            nc.sync.dma_start(out[:, outputs[h]], result[h][:])
